import numpy as np, ml_dtypes
CORES = [12,28,60,100,156,228]
N = 6
import mx_ref
NC, KT, G, ROOT = 128, 1, 2, 5
C = np.float32(0.023)
BF = ml_dtypes.bfloat16
def cut(t, i, w=512):
    return t[:, w * i:w * i + w]
def tile(rs):
    return np.stack(rs, axis=2).reshape(128, -1).astype(BF)
def layer(w, X):
    out = []
    for i in range(G):
        for t in range(len(X)):
            p = mx_ref.matmul(mx_ref.quantize(cut(w, len(X) * i + t)), X[t])
            z = p if t == 0 else z + p
        out.append(z)
    return out
def act(Z):
    return [np.maximum(s * z, 0) * C for z in Z for s in (1, -1)]
def setup_inputs(rng):
    def f(*shape):
        return mx_ref.flush((rng.standard_normal(shape, dtype=np.float32) * np.exp2(rng.integers(-2, 3, shape[:-1] + (1,)))).astype(BF))
    return {"x": f(N, 128, KT * 4 * NC), "w1": f(N, 128, G * KT * 512), "w2": f(N, 128, 512)}
def setup_inputs_blocks(rng):
    d = setup_inputs(rng)
    for k in ("x", "w1", "w2"): d[k] = mx_ref.spread(d[k], rng, 4)
    return d
def setup_inputs_wide(rng):
    d = setup_inputs(rng)
    for k in ("x", "w1", "w2"): d[k] = mx_ref.flush((d[k].astype(np.float32) * np.exp2(rng.integers(-8, 9, (N, 1, 1))).astype(np.float32)).astype(BF))
    return d
def setup_inputs_zeros(rng):
    d = setup_inputs(rng); v = d["x"].reshape(N, 128, -1, 4).copy()
    v[np.broadcast_to((rng.random((N, 1, v.shape[2], 1)) < 0.33), v.shape)] = 0
    d["x"] = v.reshape(d["x"].shape)
    return d
def reference(x, w1, w2):
    h = mx_ref.quantize(tile(act(layer(w1[ROOT], [mx_ref.quantize(cut(x[ROOT], t, 4 * NC)) for t in range(KT)]))))
    y = np.zeros((N, 128, NC), np.float32)
    for r in range(N):
        y[r] = mx_ref.matmul(mx_ref.quantize(w2[r]), h)
    return {"y": y}

@@ -1,0 +1,153 @@
+import numpy as np
+from concourse.bass import DstId, RemoteDMATransfer
+from concourse.mybir import dt, AluOpType, ActivationFunctionType
+
+WORLD = 256
+NC = 128
+C = float(np.float32(0.023))
+
+SCRATCH = {
+    "xt": ("sbuf", [128, 4 * NC], "bfloat16"),
+    "w1t": ("sbuf", [128, 1024], "bfloat16"),
+    "w2t": ("sbuf", [128, 512], "bfloat16"),
+    "ht": ("sbuf", [128, 4 * NC], "bfloat16"),
+    "qx": ("sbuf", [128, NC], "float8_e4m3fn_x4"),
+    "sx": ("sbuf", [128, NC], "uint8"),
+    "qw1": ("sbuf", [128, 256], "float8_e4m3fn_x4"),
+    "sw1": ("sbuf", [128, 256], "uint8"),
+    "qw2": ("sbuf", [128, 128], "float8_e4m3fn_x4"),
+    "sw2": ("sbuf", [128, 128], "uint8"),
+    "qh": ("sbuf", [128, NC], "float8_e4m3fn_x4"),
+    "sh": ("sbuf", [128, NC], "uint8"),
+    "z": ("psum", [128, 1024], "float32"),
+    "yp": ("psum", [128, 512], "float32"),
+    "ys": ("sbuf", [128, NC], "float32"),
+}
+SEMAPHORES = ["ldx", "ldw0", "ldw1", "ldw2", "qxd", "qw0d", "qw1d", "qw2d", "z0d", "z1d", "hs", "hv", "qhd",
+              "arr", "sent", "ypd", "ysd", "stored"]
+
+
+def _bits(mask):
+    return [b for b in range(mask.bit_length()) if (mask >> b) & 1]
+
+
+def _mask(bits):
+    m = 0
+    for b in bits:
+        m |= 1 << b
+    return m
+
+
+def _plan(T, topo):
+    root = T.cores[T.root]
+    others = [c for c in T.cores if c != root]
+    near = [c for c in others if topo.may_write(root, c)]
+    far = [c for c in others if not topo.may_write(root, c)]
+    by_die = {}
+    for c in range(WORLD):
+        if c != root and topo.host(c) == topo.host(root) and topo.chip(c) == topo.chip(root):
+            if all(topo.may_write(c, d) for d in far):
+                by_die.setdefault(topo.die(c), []).append(c)
+    pairs = [v[:2] for k, v in sorted(by_die.items(), key=lambda kv: kv[0] != topo.die(root)) if len(v) >= 2]
+    roads = [(p[0], p[1], far[i::len(pairs)]) for i, p in enumerate(pairs)]
+    return root, near, [r for r in roads if r[2]]
+
+
+def _multi(g, T, topo, core, view, dests, bits):
+    ids = []
+    for d in dests:
+        rid, pid = topo.addr(d, core)
+        ids.append(DstId(rid=rid, pnc=pid))
+    g.remote_dma_fused([RemoteDMATransfer(dst_ids=ids, dma_engine_mask=_mask(bits), remote_sem=T.sem.arr,
+                                          srcs=[view], dsts=[view for d in dests])], local_sem=T.sem.sent)
+    return len(bits)
+
+
+def _common(topo, core, dests):
+    m = topo.mask(core, dests[0])
+    for d in dests[1:]:
+        m &= topo.mask(core, d)
+    return _bits(m)
+
+
+def _second_layer(g, T, ready_sem, ready):
+    g.tensor.wait_ge(T.sem.qw2d, 1)
+    g.tensor.wait_ge(ready_sem, ready)
+    g.tensor.matmul_mx(T.yp[:, 0:NC], T.qw2[:], T.sw2[:], T.qh[:], T.sh[:], True, True).then_inc(T.sem.ypd, 1)
+    g.vector.wait_ge(T.sem.ypd, 1)
+    g.vector.tensor_copy(T.ys[:], T.yp[:, 0:NC]).then_inc(T.sem.ysd, 1)
+    g.sync.wait_ge(T.sem.ysd, 1)
+    g.sync.dma_start(T.y[:], T.ys[:]).then_inc(T.sem.stored, 16)
+    g.sync.wait_ge(T.sem.stored, 16)
+
+
+def rank_program(g, core, T, topo):
+    root, near, roads = _plan(T, topo)
+    codes = T.qh[:].bitcast(dt.uint8)
+    plane = T.sh[:]
+    code_carriers = [r[0] for r in roads]
+    plane_carriers = [r[1] for r in roads]
+    on_chip = _common(topo, root, code_carriers + plane_carriers)
+    leaving = _common(topo, root, near) if near else on_chip[:len(on_chip) // 2]
+    staying = [b for b in on_chip if b not in leaving]
+
+    for rc, rp, dests in roads:
+        if core in (rc, rp):
+            g.wait_ge(T.sem.arr, len(staying) if core == rc else len(leaving))
+            n = _multi(g, T, topo, core, codes if core == rc else plane, dests, _common(topo, core, dests))
+            g.wait_ge(T.sem.sent, n)
+            return
+
+    if T.rank_of(core) is None:
+        return
+
+    if core != root:
+        g.sync.dma_start(T.w2t[:], T.w2[:]).then_inc(T.sem.ldw2, 16)
+        g.vector.wait_ge(T.sem.ldw2, 16)
+        g.vector.quantize_mx(T.qw2[:], T.sw2[:], T.w2t[:]).then_inc(T.sem.qw2d, 1)
+        if core in near:
+            whole = 2 * len(leaving)
+        else:
+            whole = sum(len(_common(topo, c, r[2])) for r in roads if core in r[2] for c in r[:2])
+        _second_layer(g, T, T.sem.arr, whole)
+        return
+
+    g.sync.dma_start(T.xt[:], T.x[:]).then_inc(T.sem.ldx, 16)
+    g.scalar.dma_start(T.w1t[:, 0:512], T.w1[:, 0:512]).then_inc(T.sem.ldw0, 16)
+    g.sync.dma_start(T.w1t[:, 512:1024], T.w1[:, 512:1024]).then_inc(T.sem.ldw1, 16)
+    g.sync.dma_start(T.w2t[:], T.w2[:]).then_inc(T.sem.ldw2, 16)
+
+    g.vector.wait_ge(T.sem.ldx, 16)
+    g.vector.quantize_mx(T.qx[:], T.sx[:], T.xt[:]).then_inc(T.sem.qxd, 1)
+    g.vector.wait_ge(T.sem.ldw0, 16)
+    g.vector.quantize_mx(T.qw1[:, 0:128], T.sw1[:, 0:128], T.w1t[:, 0:512]).then_inc(T.sem.qw0d, 1)
+    g.vector.wait_ge(T.sem.ldw1, 16)
+    g.vector.quantize_mx(T.qw1[:, 128:256], T.sw1[:, 128:256], T.w1t[:, 512:1024]).then_inc(T.sem.qw1d, 1)
+
+    g.tensor.wait_ge(T.sem.qxd, 1)
+    g.tensor.wait_ge(T.sem.qw0d, 1)
+    g.tensor.matmul_mx(T.z[:, 0:NC], T.qw1[:, 0:128], T.sw1[:, 0:128], T.qx[:], T.sx[:], True, True).then_inc(T.sem.z0d, 1)
+    g.tensor.wait_ge(T.sem.qw1d, 1)
+    g.tensor.matmul_mx(T.z[:, 512:512 + NC], T.qw1[:, 128:256], T.sw1[:, 128:256], T.qx[:], T.sx[:], True, True).then_inc(T.sem.z1d, 1)
+
+    g.scalar.wait_ge(T.sem.z0d, 1)
+    g.scalar.activation(T.ht[:, 0:4 * NC:4], T.z[:, 0:NC], ActivationFunctionType.Relu, scale=C).then_inc(T.sem.hs, 1)
+    g.scalar.activation(T.ht[:, 1:4 * NC:4], T.z[:, 0:NC], ActivationFunctionType.Relu, scale=-C).then_inc(T.sem.hs, 1)
+    g.vector.wait_ge(T.sem.z1d, 1)
+    g.vector.tensor_scalar(T.ht[:, 2:4 * NC:4], T.z[:, 512:512 + NC], 0.0, C, AluOpType.max, AluOpType.mult).then_inc(T.sem.hv, 1)
+    g.vector.tensor_scalar(T.ht[:, 3:4 * NC:4], T.z[:, 512:512 + NC], -C, 0.0, AluOpType.mult, AluOpType.max).then_inc(T.sem.hv, 1)
+    g.vector.wait_ge(T.sem.hs, 2)
+    g.vector.wait_ge(T.sem.hv, 2)
+    g.vector.quantize_mx(T.qh[:], T.sh[:], T.ht[:]).then_inc(T.sem.qhd, 1)
+    g.vector.wait_ge(T.sem.ldw2, 16)
+    g.vector.quantize_mx(T.qw2[:], T.sw2[:], T.w2t[:]).then_inc(T.sem.qw2d, 1)
+
+    g.wait_ge(T.sem.qhd, 1)
+    n = _multi(g, T, topo, core, codes, code_carriers, staying)
+    n += _multi(g, T, topo, core, plane, plane_carriers, leaving)
+    if near:
+        n += _multi(g, T, topo, core, codes, near, leaving)
+        n += _multi(g, T, topo, core, plane, near, leaving)
+
+    _second_layer(g, T, T.sem.qhd, 1)
+    g.wait_ge(T.sem.sent, n)

@@ -11,10 +11,8 @@ SCRATCH = {
     "w1t": ("sbuf", [128, 1024], "bfloat16"),
     "w2t": ("sbuf", [128, 512], "bfloat16"),
     "ht": ("sbuf", [128, 4 * NC], "bfloat16"),
-    "qx": ("sbuf", [128, NC], "float8_e4m3fn_x4"),
-    "sx": ("sbuf", [128, NC], "uint8"),
-    "qw1": ("sbuf", [128, 256], "float8_e4m3fn_x4"),
-    "sw1": ("sbuf", [128, 256], "uint8"),
+    "qa": ("sbuf", [128, 3 * NC], "float8_e4m3fn_x4"),
+    "sa": ("sbuf", [128, 3 * NC], "uint8"),
     "qw2": ("sbuf", [128, 128], "float8_e4m3fn_x4"),
     "sw2": ("sbuf", [128, 128], "uint8"),
     "qh": ("sbuf", [128, NC], "float8_e4m3fn_x4"),
@@ -24,7 +22,7 @@ SCRATCH = {
     "ys": ("sbuf", [128, NC], "float32"),
 }
 SEMAPHORES = ["ldx", "ldw0", "ldw1", "ldw2", "qxd", "qw0d", "qw1d", "qw2d", "z0d", "z1d", "hs", "hv", "qhd",
-              "arr", "sent", "ypd", "ysd", "stored"]
+              "arr", "arrp", "arrc", "sent", "ypd", "ysd", "stored"]
 
 
 def _bits(mask):
@@ -43,22 +41,20 @@ def _plan(T, topo):
     others = [c for c in T.cores if c != root]
     near = [c for c in others if topo.may_write(root, c)]
     far = [c for c in others if not topo.may_write(root, c)]
-    by_die = {}
-    for c in range(WORLD):
-        if c != root and topo.host(c) == topo.host(root) and topo.chip(c) == topo.chip(root):
-            if all(topo.may_write(c, d) for d in far):
-                by_die.setdefault(topo.die(c), []).append(c)
-    pairs = [v[:2] for k, v in sorted(by_die.items(), key=lambda kv: kv[0] != topo.die(root)) if len(v) >= 2]
-    roads = [(p[0], p[1], far[i::len(pairs)]) for i, p in enumerate(pairs)]
-    return root, near, [r for r in roads if r[2]]
+    carriers = [c for c in range(WORLD)
+                if c != root and topo.host(c) == topo.host(root) and topo.chip(c) == topo.chip(root)
+                and all(topo.may_write(c, d) for d in far)]
+    carriers.sort(key=lambda c: (topo.die(c) != topo.die(root), c))
+    roads = [(c, far[i::len(carriers)]) for i, c in enumerate(carriers)]
+    return root, near, [r for r in roads if r[1]]
 
 
-def _multi(g, T, topo, core, view, dests, bits):
+def _multi(g, T, topo, core, view, dests, bits, sem):
     ids = []
     for d in dests:
         rid, pid = topo.addr(d, core)
         ids.append(DstId(rid=rid, pnc=pid))
-    g.remote_dma_fused([RemoteDMATransfer(dst_ids=ids, dma_engine_mask=_mask(bits), remote_sem=T.sem.arr,
+    g.remote_dma_fused([RemoteDMATransfer(dst_ids=ids, dma_engine_mask=_mask(bits), remote_sem=sem,
                                           srcs=[view], dsts=[view for d in dests])], local_sem=T.sem.sent)
     return len(bits)
 
@@ -68,6 +64,24 @@ def _common(topo, core, dests):
     for d in dests[1:]:
         m &= topo.mask(core, d)
     return _bits(m)
+
+
+def _first_layer(g, T, before0, before1):
+    for s, v in before0:
+        g.tensor.wait_ge(s, v)
+    g.tensor.matmul_mx(T.z[:, 0:NC], T.qa[:, NC:2 * NC], T.sa[:, NC:2 * NC], T.qa[:, 0:NC], T.sa[:, 0:NC], True, True).then_inc(T.sem.z0d, 1)
+    for s, v in before1:
+        g.tensor.wait_ge(s, v)
+    g.tensor.matmul_mx(T.z[:, 512:512 + NC], T.qa[:, 2 * NC:3 * NC], T.sa[:, 2 * NC:3 * NC], T.qa[:, 0:NC], T.sa[:, 0:NC], True, True).then_inc(T.sem.z1d, 1)
+    g.scalar.wait_ge(T.sem.z0d, 1)
+    g.scalar.activation(T.ht[:, 0:4 * NC:4], T.z[:, 0:NC], ActivationFunctionType.Relu, scale=C).then_inc(T.sem.hs, 1)
+    g.scalar.activation(T.ht[:, 1:4 * NC:4], T.z[:, 0:NC], ActivationFunctionType.Relu, scale=-C).then_inc(T.sem.hs, 1)
+    g.vector.wait_ge(T.sem.z1d, 1)
+    g.vector.tensor_scalar(T.ht[:, 2:4 * NC:4], T.z[:, 512:512 + NC], 0.0, C, AluOpType.max, AluOpType.mult).then_inc(T.sem.hv, 1)
+    g.vector.tensor_scalar(T.ht[:, 3:4 * NC:4], T.z[:, 512:512 + NC], -C, 0.0, AluOpType.mult, AluOpType.max).then_inc(T.sem.hv, 1)
+    g.vector.wait_ge(T.sem.hs, 2)
+    g.vector.wait_ge(T.sem.hv, 2)
+    g.vector.quantize_mx(T.qh[:], T.sh[:], T.ht[:]).then_inc(T.sem.qhd, 1)
 
 
 def _second_layer(g, T, ready_sem, ready):
@@ -85,16 +99,18 @@ def rank_program(g, core, T, topo):
     root, near, roads = _plan(T, topo)
     codes = T.qh[:].bitcast(dt.uint8)
     plane = T.sh[:]
-    code_carriers = [r[0] for r in roads]
-    plane_carriers = [r[1] for r in roads]
-    on_chip = _common(topo, root, code_carriers + plane_carriers)
-    leaving = _common(topo, root, near) if near else on_chip[:len(on_chip) // 2]
+    carriers = [r[0] for r in roads]
+    on_chip = _common(topo, root, carriers)
+    leaving = _common(topo, root, near)
     staying = [b for b in on_chip if b not in leaving]
 
-    for rc, rp, dests in roads:
-        if core in (rc, rp):
-            g.wait_ge(T.sem.arr, len(staying) if core == rc else len(leaving))
-            n = _multi(g, T, topo, core, codes if core == rc else plane, dests, _common(topo, core, dests))
+    for c, dests in roads:
+        if core == c:
+            out = _common(topo, core, dests)
+            g.wait_ge(T.sem.arrp, len(leaving))
+            n = _multi(g, T, topo, core, plane, dests, out, T.sem.arr)
+            g.wait_ge(T.sem.arrc, len(staying))
+            n += _multi(g, T, topo, core, codes, dests, out, T.sem.arr)
             g.wait_ge(T.sem.sent, n)
             return
 
@@ -106,10 +122,11 @@ def rank_program(g, core, T, topo):
         g.vector.wait_ge(T.sem.ldw2, 16)
         g.vector.quantize_mx(T.qw2[:], T.sw2[:], T.w2t[:]).then_inc(T.sem.qw2d, 1)
         if core in near:
-            whole = 2 * len(leaving)
+            _first_layer(g, T, [(T.sem.arr, 3 * len(leaving))], [])
+            _second_layer(g, T, T.sem.qhd, 1)
         else:
-            whole = sum(len(_common(topo, c, r[2])) for r in roads if core in r[2] for c in r[:2])
-        _second_layer(g, T, T.sem.arr, whole)
+            whole = sum(2 * len(_common(topo, c, d)) for c, d in roads if core in d)
+            _second_layer(g, T, T.sem.arr, whole)
         return
 
     g.sync.dma_start(T.xt[:], T.x[:]).then_inc(T.sem.ldx, 16)
@@ -118,36 +135,25 @@ def rank_program(g, core, T, topo):
     g.sync.dma_start(T.w2t[:], T.w2[:]).then_inc(T.sem.ldw2, 16)
 
     g.vector.wait_ge(T.sem.ldx, 16)
-    g.vector.quantize_mx(T.qx[:], T.sx[:], T.xt[:]).then_inc(T.sem.qxd, 1)
+    g.vector.quantize_mx(T.qa[:, 0:NC], T.sa[:, 0:NC], T.xt[:]).then_inc(T.sem.qxd, 1)
     g.vector.wait_ge(T.sem.ldw0, 16)
-    g.vector.quantize_mx(T.qw1[:, 0:128], T.sw1[:, 0:128], T.w1t[:, 0:512]).then_inc(T.sem.qw0d, 1)
+    g.vector.quantize_mx(T.qa[:, NC:2 * NC], T.sa[:, NC:2 * NC], T.w1t[:, 0:512]).then_inc(T.sem.qw0d, 1)
     g.vector.wait_ge(T.sem.ldw1, 16)
-    g.vector.quantize_mx(T.qw1[:, 128:256], T.sw1[:, 128:256], T.w1t[:, 512:1024]).then_inc(T.sem.qw1d, 1)
+    g.vector.quantize_mx(T.qa[:, 2 * NC:3 * NC], T.sa[:, 2 * NC:3 * NC], T.w1t[:, 512:1024]).then_inc(T.sem.qw1d, 1)
 
-    g.tensor.wait_ge(T.sem.qxd, 1)
-    g.tensor.wait_ge(T.sem.qw0d, 1)
-    g.tensor.matmul_mx(T.z[:, 0:NC], T.qw1[:, 0:128], T.sw1[:, 0:128], T.qx[:], T.sx[:], True, True).then_inc(T.sem.z0d, 1)
-    g.tensor.wait_ge(T.sem.qw1d, 1)
-    g.tensor.matmul_mx(T.z[:, 512:512 + NC], T.qw1[:, 128:256], T.sw1[:, 128:256], T.qx[:], T.sx[:], True, True).then_inc(T.sem.z1d, 1)
-
-    g.scalar.wait_ge(T.sem.z0d, 1)
-    g.scalar.activation(T.ht[:, 0:4 * NC:4], T.z[:, 0:NC], ActivationFunctionType.Relu, scale=C).then_inc(T.sem.hs, 1)
-    g.scalar.activation(T.ht[:, 1:4 * NC:4], T.z[:, 0:NC], ActivationFunctionType.Relu, scale=-C).then_inc(T.sem.hs, 1)
-    g.vector.wait_ge(T.sem.z1d, 1)
-    g.vector.tensor_scalar(T.ht[:, 2:4 * NC:4], T.z[:, 512:512 + NC], 0.0, C, AluOpType.max, AluOpType.mult).then_inc(T.sem.hv, 1)
-    g.vector.tensor_scalar(T.ht[:, 3:4 * NC:4], T.z[:, 512:512 + NC], -C, 0.0, AluOpType.mult, AluOpType.max).then_inc(T.sem.hv, 1)
-    g.vector.wait_ge(T.sem.hs, 2)
-    g.vector.wait_ge(T.sem.hv, 2)
-    g.vector.quantize_mx(T.qh[:], T.sh[:], T.ht[:]).then_inc(T.sem.qhd, 1)
+    _first_layer(g, T, [(T.sem.qxd, 1), (T.sem.qw0d, 1)], [(T.sem.qw1d, 1)])
     g.vector.wait_ge(T.sem.ldw2, 16)
     g.vector.quantize_mx(T.qw2[:], T.sw2[:], T.w2t[:]).then_inc(T.sem.qw2d, 1)
 
+    g.wait_ge(T.sem.qxd, 1)
+    n = _multi(g, T, topo, core, T.sa[:, 0:NC], near, leaving, T.sem.arr)
     g.wait_ge(T.sem.qhd, 1)
-    n = _multi(g, T, topo, core, codes, code_carriers, staying)
-    n += _multi(g, T, topo, core, plane, plane_carriers, leaving)
-    if near:
-        n += _multi(g, T, topo, core, codes, near, leaving)
-        n += _multi(g, T, topo, core, plane, near, leaving)
+    n += _multi(g, T, topo, core, plane, carriers, leaving, T.sem.arrp)
+    n += _multi(g, T, topo, core, codes, carriers, staying, T.sem.arrc)
+    g.wait_ge(T.sem.qw0d, 1)
+    g.wait_ge(T.sem.qw1d, 1)
+    n += _multi(g, T, topo, core, T.qa[:].bitcast(dt.uint8), near, leaving, T.sem.arr)
+    n += _multi(g, T, topo, core, T.sa[:, NC:3 * NC], near, leaving, T.sem.arr)
 
     _second_layer(g, T, T.sem.qhd, 1)
     g.wait_ge(T.sem.sent, n)

@@ -22,7 +22,7 @@ SCRATCH = {
     "ys": ("sbuf", [128, NC], "float32"),
 }
 SEMAPHORES = ["ldx", "ldw0", "ldw1", "ldw2", "qxd", "qw0d", "qw1d", "qw2d", "z0d", "z1d", "hs", "hv", "qhd",
-              "arr", "arrp", "arrc", "sent", "ypd", "ysd", "stored"]
+              "arr", "arrx", "arrp", "arrc", "sent", "ypd", "ysd", "stored"]
 
 
 def _bits(mask):
@@ -46,16 +46,19 @@ def _plan(T, topo):
                 and all(topo.may_write(c, d) for d in far)]
     carriers.sort(key=lambda c: (topo.die(c) != topo.die(root), c))
     roads = [(c, far[i::len(carriers)]) for i, c in enumerate(carriers)]
-    return root, near, [r for r in roads if r[1]]
+    return root, near, far, [r for r in roads if r[1]]
 
 
-def _multi(g, T, topo, core, view, dests, bits, sem):
+def _transfer(topo, core, view, dests, bits, sem):
     ids = []
     for d in dests:
         rid, pid = topo.addr(d, core)
         ids.append(DstId(rid=rid, pnc=pid))
-    g.remote_dma_fused([RemoteDMATransfer(dst_ids=ids, dma_engine_mask=_mask(bits), remote_sem=sem,
-                                          srcs=[view], dsts=[view for d in dests])], local_sem=T.sem.sent)
+    return RemoteDMATransfer(dst_ids=ids, dma_engine_mask=_mask(bits), remote_sem=sem, srcs=[view], dsts=[view for d in dests])
+
+
+def _multi(g, T, topo, core, view, dests, bits, sem):
+    g.remote_dma_fused([_transfer(topo, core, view, dests, bits, sem)], local_sem=T.sem.sent)
     return len(bits)
 
 
@@ -96,21 +99,30 @@ def _second_layer(g, T, ready_sem, ready):
 
 
 def rank_program(g, core, T, topo):
-    root, near, roads = _plan(T, topo)
+    root, near, far, roads = _plan(T, topo)
     codes = T.qh[:].bitcast(dt.uint8)
     plane = T.sh[:]
     carriers = [r[0] for r in roads]
     on_chip = _common(topo, root, carriers)
     leaving = _common(topo, root, near)
     staying = [b for b in on_chip if b not in leaving]
+    bulk, brief = leaving[0::2], leaving[1::2]
+    per = len(on_chip) // len(carriers)
+    QW = NC // 4
+    pieces = ([T.sa[:, 0:NC]] + [T.qa[:, k * QW:(k + 1) * QW].bitcast(dt.uint8) for k in range(4)])[:len(carriers)]
+    direct = (len(pieces) - 1) * QW
+    pl = [c for c in carriers if topo.die(c) == topo.die(root)]
+    planes_of = {c: far[j::len(pl)] for j, c in enumerate(pl)}
 
-    for c, dests in roads:
+    for i, (c, dests) in enumerate(roads):
         if core == c:
-            out = _common(topo, core, dests)
-            g.wait_ge(T.sem.arrp, len(leaving))
-            n = _multi(g, T, topo, core, plane, dests, out, T.sem.arr)
+            g.wait_ge(T.sem.arrx, per)
+            n = _multi(g, T, topo, core, pieces[i], near, _common(topo, core, near), T.sem.arr)
+            if c in planes_of:
+                g.wait_ge(T.sem.arrp, len(brief))
+                n += _multi(g, T, topo, core, plane, planes_of[c], _common(topo, core, planes_of[c]), T.sem.arr)
             g.wait_ge(T.sem.arrc, len(staying))
-            n += _multi(g, T, topo, core, codes, dests, out, T.sem.arr)
+            n += _multi(g, T, topo, core, codes, dests, _common(topo, core, dests), T.sem.arr)
             g.wait_ge(T.sem.sent, n)
             return
 
@@ -122,10 +134,12 @@ def rank_program(g, core, T, topo):
         g.vector.wait_ge(T.sem.ldw2, 16)
         g.vector.quantize_mx(T.qw2[:], T.sw2[:], T.w2t[:]).then_inc(T.sem.qw2d, 1)
         if core in near:
-            _first_layer(g, T, [(T.sem.arr, 3 * len(leaving))], [])
+            whole = sum(len(_common(topo, c, near)) for c in carriers) + len(bulk) + 2 * len(leaving)
+            _first_layer(g, T, [(T.sem.arr, whole)], [])
             _second_layer(g, T, T.sem.qhd, 1)
         else:
-            whole = sum(2 * len(_common(topo, c, d)) for c, d in roads if core in d)
+            whole = sum(len(_common(topo, c, d)) for c, d in roads if core in d)
+            whole += sum(len(_common(topo, c, d)) for c, d in planes_of.items() if core in d)
             _second_layer(g, T, T.sem.arr, whole)
         return
 
@@ -146,13 +160,16 @@ def rank_program(g, core, T, topo):
     g.vector.quantize_mx(T.qw2[:], T.sw2[:], T.w2t[:]).then_inc(T.sem.qw2d, 1)
 
     g.wait_ge(T.sem.qxd, 1)
-    n = _multi(g, T, topo, core, T.sa[:, 0:NC], near, leaving, T.sem.arr)
-    g.wait_ge(T.sem.qhd, 1)
-    n += _multi(g, T, topo, core, plane, carriers, leaving, T.sem.arrp)
-    n += _multi(g, T, topo, core, codes, carriers, staying, T.sem.arrc)
+    g.remote_dma_fused([_transfer(topo, core, pieces[i], [c], on_chip[i * per:(i + 1) * per], T.sem.arrx)
+                        for i, c in enumerate(carriers)], local_sem=T.sem.sent)
+    n = per * len(carriers)
     g.wait_ge(T.sem.qw0d, 1)
+    n += _multi(g, T, topo, core, T.qa[:, direct:2 * NC].bitcast(dt.uint8), near, bulk, T.sem.arr)
+    g.wait_ge(T.sem.qhd, 1)
+    n += _multi(g, T, topo, core, plane, pl, brief, T.sem.arrp)
+    n += _multi(g, T, topo, core, codes, carriers, staying, T.sem.arrc)
     g.wait_ge(T.sem.qw1d, 1)
-    n += _multi(g, T, topo, core, T.qa[:].bitcast(dt.uint8), near, leaving, T.sem.arr)
+    n += _multi(g, T, topo, core, T.qa[:, 2 * NC:3 * NC].bitcast(dt.uint8), near, leaving, T.sem.arr)
     n += _multi(g, T, topo, core, T.sa[:, NC:3 * NC], near, leaving, T.sem.arr)
 
     _second_layer(g, T, T.sem.qhd, 1)

import numpy as np
from concourse.bass import DstId, RemoteDMATransfer
from concourse.mybir import dt, AluOpType, ActivationFunctionType

WORLD = 256
NC = 128
C = float(np.float32(0.023))

SCRATCH = {
    "xt": ("sbuf", [128, 4 * NC], "bfloat16"),
    "w1t": ("sbuf", [128, 1024], "bfloat16"),
    "w2t": ("sbuf", [128, 512], "bfloat16"),
    "ht": ("sbuf", [128, 4 * NC], "bfloat16"),
    "qa": ("sbuf", [128, 3 * NC], "float8_e4m3fn_x4"),
    "sa": ("sbuf", [128, 3 * NC], "uint8"),
    "qw2": ("sbuf", [128, 128], "float8_e4m3fn_x4"),
    "sw2": ("sbuf", [128, 128], "uint8"),
    "qh": ("sbuf", [128, NC], "float8_e4m3fn_x4"),
    "sh": ("sbuf", [128, NC], "uint8"),
    "z": ("psum", [128, 1024], "float32"),
    "yp": ("psum", [128, 512], "float32"),
    "ys": ("sbuf", [128, NC], "float32"),
}
SEMAPHORES = ["ldx", "ldw0", "ldw1", "ldw2", "qxd", "qw0d", "qw1d", "qw2d", "z0d", "z1d", "hs", "hv", "qhd",
              "arr", "arrx", "arrp", "arrc", "sent", "ypd", "ysd", "stored"]


def _bits(mask):
    return [b for b in range(mask.bit_length()) if (mask >> b) & 1]


def _mask(bits):
    m = 0
    for b in bits:
        m |= 1 << b
    return m


def _plan(T, topo):
    root = T.cores[T.root]
    others = [c for c in T.cores if c != root]
    near = [c for c in others if topo.may_write(root, c)]
    far = [c for c in others if not topo.may_write(root, c)]
    carriers = [c for c in range(WORLD)
                if c != root and topo.host(c) == topo.host(root) and topo.chip(c) == topo.chip(root)
                and all(topo.may_write(c, d) for d in far)]
    carriers.sort(key=lambda c: (topo.die(c) != topo.die(root), c))
    roads = [(c, far[i::len(carriers)]) for i, c in enumerate(carriers)]
    return root, near, far, [r for r in roads if r[1]]


def _transfer(topo, core, view, dests, bits, sem):
    ids = []
    for d in dests:
        rid, pid = topo.addr(d, core)
        ids.append(DstId(rid=rid, pnc=pid))
    return RemoteDMATransfer(dst_ids=ids, dma_engine_mask=_mask(bits), remote_sem=sem, srcs=[view], dsts=[view for d in dests])


def _multi(g, T, topo, core, view, dests, bits, sem):
    g.remote_dma_fused([_transfer(topo, core, view, dests, bits, sem)], local_sem=T.sem.sent)
    return len(bits)


def _common(topo, core, dests):
    m = topo.mask(core, dests[0])
    for d in dests[1:]:
        m &= topo.mask(core, d)
    return _bits(m)


def _first_layer(g, T, before0, before1):
    for s, v in before0:
        g.tensor.wait_ge(s, v)
    g.tensor.matmul_mx(T.z[:, 0:NC], T.qa[:, NC:2 * NC], T.sa[:, NC:2 * NC], T.qa[:, 0:NC], T.sa[:, 0:NC], True, True).then_inc(T.sem.z0d, 1)
    for s, v in before1:
        g.tensor.wait_ge(s, v)
    g.tensor.matmul_mx(T.z[:, 512:512 + NC], T.qa[:, 2 * NC:3 * NC], T.sa[:, 2 * NC:3 * NC], T.qa[:, 0:NC], T.sa[:, 0:NC], True, True).then_inc(T.sem.z1d, 1)
    g.scalar.wait_ge(T.sem.z0d, 1)
    g.scalar.activation(T.ht[:, 0:4 * NC:4], T.z[:, 0:NC], ActivationFunctionType.Relu, scale=C).then_inc(T.sem.hs, 1)
    g.scalar.activation(T.ht[:, 1:4 * NC:4], T.z[:, 0:NC], ActivationFunctionType.Relu, scale=-C).then_inc(T.sem.hs, 1)
    g.vector.wait_ge(T.sem.z1d, 1)
    g.vector.tensor_scalar(T.ht[:, 2:4 * NC:4], T.z[:, 512:512 + NC], 0.0, C, AluOpType.max, AluOpType.mult).then_inc(T.sem.hv, 1)
    g.vector.tensor_scalar(T.ht[:, 3:4 * NC:4], T.z[:, 512:512 + NC], -C, 0.0, AluOpType.mult, AluOpType.max).then_inc(T.sem.hv, 1)
    g.vector.wait_ge(T.sem.hs, 2)
    g.vector.wait_ge(T.sem.hv, 2)
    g.vector.quantize_mx(T.qh[:], T.sh[:], T.ht[:]).then_inc(T.sem.qhd, 1)


def _second_layer(g, T, ready_sem, ready):
    g.tensor.wait_ge(T.sem.qw2d, 1)
    g.tensor.wait_ge(ready_sem, ready)
    g.tensor.matmul_mx(T.yp[:, 0:NC], T.qw2[:], T.sw2[:], T.qh[:], T.sh[:], True, True).then_inc(T.sem.ypd, 1)
    g.vector.wait_ge(T.sem.ypd, 1)
    g.vector.tensor_copy(T.ys[:], T.yp[:, 0:NC]).then_inc(T.sem.ysd, 1)
    g.sync.wait_ge(T.sem.ysd, 1)
    g.sync.dma_start(T.y[:], T.ys[:]).then_inc(T.sem.stored, 16)
    g.sync.wait_ge(T.sem.stored, 16)


def rank_program(g, core, T, topo):
    root, near, far, roads = _plan(T, topo)
    codes = T.qh[:].bitcast(dt.uint8)
    plane = T.sh[:]
    carriers = [r[0] for r in roads]
    on_chip = _common(topo, root, carriers)
    leaving = _common(topo, root, near)
    staying = [b for b in on_chip if b not in leaving]
    bulk, brief = leaving[0::2], leaving[1::2]
    per = len(on_chip) // len(carriers)
    QW = NC // 4
    pieces = ([T.sa[:, 0:NC]] + [T.qa[:, k * QW:(k + 1) * QW].bitcast(dt.uint8) for k in range(4)])[:len(carriers)]
    direct = (len(pieces) - 1) * QW
    pl = [c for c in carriers if topo.die(c) == topo.die(root)]
    planes_of = {c: far[j::len(pl)] for j, c in enumerate(pl)}

    for i, (c, dests) in enumerate(roads):
        if core == c:
            g.wait_ge(T.sem.arrx, per)
            n = _multi(g, T, topo, core, pieces[i], near, _common(topo, core, near), T.sem.arr)
            if c in planes_of:
                g.wait_ge(T.sem.arrp, len(brief))
                n += _multi(g, T, topo, core, plane, planes_of[c], _common(topo, core, planes_of[c]), T.sem.arr)
            g.wait_ge(T.sem.arrc, len(staying))
            n += _multi(g, T, topo, core, codes, dests, _common(topo, core, dests), T.sem.arr)
            g.wait_ge(T.sem.sent, n)
            return

    if T.rank_of(core) is None:
        return

    if core != root:
        g.sync.dma_start(T.w2t[:], T.w2[:]).then_inc(T.sem.ldw2, 16)
        g.vector.wait_ge(T.sem.ldw2, 16)
        g.vector.quantize_mx(T.qw2[:], T.sw2[:], T.w2t[:]).then_inc(T.sem.qw2d, 1)
        if core in near:
            whole = sum(len(_common(topo, c, near)) for c in carriers) + len(bulk) + 2 * len(leaving)
            _first_layer(g, T, [(T.sem.arr, whole)], [])
            _second_layer(g, T, T.sem.qhd, 1)
        else:
            whole = sum(len(_common(topo, c, d)) for c, d in roads if core in d)
            whole += sum(len(_common(topo, c, d)) for c, d in planes_of.items() if core in d)
            _second_layer(g, T, T.sem.arr, whole)
        return

    g.sync.dma_start(T.xt[:], T.x[:]).then_inc(T.sem.ldx, 16)
    g.scalar.dma_start(T.w1t[:, 0:512], T.w1[:, 0:512]).then_inc(T.sem.ldw0, 16)
    g.sync.dma_start(T.w1t[:, 512:1024], T.w1[:, 512:1024]).then_inc(T.sem.ldw1, 16)
    g.sync.dma_start(T.w2t[:], T.w2[:]).then_inc(T.sem.ldw2, 16)

    g.vector.wait_ge(T.sem.ldx, 16)
    g.vector.quantize_mx(T.qa[:, 0:NC], T.sa[:, 0:NC], T.xt[:]).then_inc(T.sem.qxd, 1)
    g.vector.wait_ge(T.sem.ldw0, 16)
    g.vector.quantize_mx(T.qa[:, NC:2 * NC], T.sa[:, NC:2 * NC], T.w1t[:, 0:512]).then_inc(T.sem.qw0d, 1)
    g.vector.wait_ge(T.sem.ldw1, 16)
    g.vector.quantize_mx(T.qa[:, 2 * NC:3 * NC], T.sa[:, 2 * NC:3 * NC], T.w1t[:, 512:1024]).then_inc(T.sem.qw1d, 1)

    _first_layer(g, T, [(T.sem.qxd, 1), (T.sem.qw0d, 1)], [(T.sem.qw1d, 1)])
    g.vector.wait_ge(T.sem.ldw2, 16)
    g.vector.quantize_mx(T.qw2[:], T.sw2[:], T.w2t[:]).then_inc(T.sem.qw2d, 1)

    g.wait_ge(T.sem.qxd, 1)
    g.remote_dma_fused([_transfer(topo, core, pieces[i], [c], on_chip[i * per:(i + 1) * per], T.sem.arrx)
                        for i, c in enumerate(carriers)], local_sem=T.sem.sent)
    n = per * len(carriers)
    g.wait_ge(T.sem.qw0d, 1)
    n += _multi(g, T, topo, core, T.qa[:, direct:2 * NC].bitcast(dt.uint8), near, bulk, T.sem.arr)
    g.wait_ge(T.sem.qhd, 1)
    n += _multi(g, T, topo, core, plane, pl, brief, T.sem.arrp)
    n += _multi(g, T, topo, core, codes, carriers, staying, T.sem.arrc)
    g.wait_ge(T.sem.qw1d, 1)
    n += _multi(g, T, topo, core, T.qa[:, 2 * NC:3 * NC].bitcast(dt.uint8), near, leaving, T.sem.arr)
    n += _multi(g, T, topo, core, T.sa[:, NC:3 * NC], near, leaving, T.sem.arr)

    _second_layer(g, T, T.sem.qhd, 1)
    g.wait_ge(T.sem.sent, n)
